import numpy as np
import ml_dtypes


def mxq(x, axis, fmt="e4m3"):
    dtype, down = {"e4m3": (ml_dtypes.float8_e4m3fn, 7), "e5m2": (ml_dtypes.float8_e5m2, 14)}[fmt]
    v = np.moveaxis(np.asarray(x, np.float32).astype(ml_dtypes.bfloat16).astype(np.float64), axis, -1)
    blocks = v.reshape(v.shape[:-1] + (-1, 32))
    amax = np.abs(blocks).max(-1, keepdims=True)
    byte = np.maximum(np.where(amax > 0, np.frexp(amax)[1] - 1 + 127, 0) - down, 1)
    scale = np.exp2(byte - 127.0)
    codes = (blocks / scale).astype(np.float32).astype(dtype).astype(np.float64)
    return np.moveaxis((codes * scale).reshape(v.shape), -1, axis)


WIDE = False


def mx_kscale(k):
    if not WIDE:
        return np.ones(k)
    levels = np.array([30, -30])
    if k % 512:
        return np.exp2(np.random.permutation(np.resize(levels, k // 32))).repeat(32)
    a = np.empty((k // 512, 16))
    for p in range(k // 512):
        a[p, :8] = np.random.permutation(np.resize(levels, 8))
        for g in range(8):
            far = levels[np.abs(levels - a[p, g]) >= 10]
            a[p, g + 8] = far[np.random.randint(len(far))]
    return np.exp2(a.ravel()).repeat(32)


def f64(x):
    return np.asarray(x).astype(np.float64)


def striped(idx):
    return np.tile(np.asarray(idx).reshape(-1, 16).T, (8, 1)).astype(np.uint16)


def unstriped(offs):
    return offs[:16].T.reshape(-1).astype(np.int64)


E2M1 = np.array([0.0, 0.5, 1.0, 1.5, 2.0, 3.0, 4.0, 6.0, -0.0, -0.5, -1.0, -1.5, -2.0, -3.0, -4.0, -6.0])


def pack_weight(w, fmt):
    k, n = w.shape
    w = f64(np.asarray(w, np.float32).astype(ml_dtypes.bfloat16)).reshape(k // 32, 32, n)
    amax = np.abs(w).max(1)
    if fmt in ("e4m3", "e5m2"):
        byte = np.frexp(amax)[1] - 1 + 127 - (7 if fmt == "e4m3" else 14)
    else:
        mant, ex = np.frexp(amax / 6.0)
        byte = np.where(mant > 0.5, ex, ex - 1) + 127
    byte = np.clip(np.where(amax > 0, byte, 1), 1, 254)
    scaled = (w * np.exp2(127.0 - byte)[:, None, :]).reshape(k, n).astype(np.float32)
    by_word = np.ascontiguousarray(scaled.reshape(k // 512, 128, 4, n).transpose(0, 1, 3, 2))
    if fmt in ("e4m3", "e5m2"):
        words = by_word.astype(ml_dtypes.float8_e4m3fn if fmt == "e4m3" else ml_dtypes.float8_e5m2).view(np.uint8)
    else:
        c = by_word.astype(ml_dtypes.float4_e2m1fn).view(np.uint8) & 0xF
        words = (c[..., 0::2] | (c[..., 1::2] << 4)).reshape(k // 512, 128, 2 * n)
    return np.ascontiguousarray(words), np.ascontiguousarray(byte.astype(np.uint8).reshape(k // 512, 16, n))


def unpack_weight(words, scales, fmt):
    g, _, n = scales.shape
    words = np.ascontiguousarray(words).reshape(g, 128, n, -1)
    if fmt in ("e4m3", "e5m2"):
        vals = words.view(ml_dtypes.float8_e4m3fn if fmt == "e4m3" else ml_dtypes.float8_e5m2).astype(np.float64)
    else:
        nib = np.empty((g, 128, n, 4), np.uint8)
        nib[..., 0::2] = words & 0xF
        nib[..., 1::2] = words >> 4
        vals = E2M1[nib]
    vals = vals * np.repeat(np.exp2(scales.astype(np.float64) - 127.0), 8, axis=1)[..., None]
    return vals.transpose(0, 1, 3, 2).reshape(g * 512, n)


K, T, J, R, L, N = 1024, 1024, 256, 512, 512, 256


def setup_inputs():
    n = np.random.standard_normal
    idx = np.random.permutation(T)[:J]
    idx2 = np.random.permutation(T)[:J]
    fk = mx_kscale(K)
    fr = mx_kscale(R)
    fl = mx_kscale(L)
    sxp = pack_weight(n((L, J)) / fl[:, None], "e5m2")
    wsp = pack_weight(n((L, R)) * 1 / np.sqrt(L) * fl[:, None] * fr, "e5m2")
    wbp = pack_weight(n((R, N)) * 1 / np.sqrt(R) / fr[:, None], "e2m1")
    return {
        "xf": (n((K, T))).astype(np.float32),
        "fk": (np.random.uniform(0.5, 2.0, (K, 1)) / fk[:, None]).astype(np.float32),
        "w": (n((K, R)) * 1 / np.sqrt(K) * fk[:, None] * fr).astype(np.float32),
        "sx_words": sxp[0],
        "sx_scales": sxp[1],
        "ws_words": wsp[0],
        "ws_scales": wsp[1],
        "wb_words": wbp[0],
        "wb_scales": wbp[1],
        "bi": (np.random.uniform(-0.5, 0.5, (1, N))).astype(np.float32),
        "offs": striped(idx),
        "offs2": striped(idx2),
    }


def reference(xf, fk, w, sx_words, sx_scales, ws_words, ws_scales, wb_words, wb_scales, bi, offs, offs2):
    idx = unstriped(offs)
    idx2 = unstriped(offs2)
    sxu = unpack_weight(sx_words, sx_scales, "e5m2")
    wsu = unpack_weight(ws_words, ws_scales, "e5m2")
    wbu = unpack_weight(wb_words, wb_scales, "e2m1")
    u = np.maximum(f64(xf)[:, idx], f64(xf)[:, idx2]) * f64(fk)
    wq = mxq(f64(w), 0, "e5m2")
    uq = mxq(u, 0, "e4m3")
    a = wq.T @ uq
    b2 = wsu.T @ sxu
    hid = np.maximum(a, b2)
    hidq = mxq(hid, 0, "e5m2")
    p = hidq.T @ wbu
    ea = np.exp(0.7 * p + f64(bi))
    y = 256.0 * ea / np.sum(ea, axis=1, keepdims=True)
    return y

@@ -1,0 +1,242 @@
+from contextlib import ExitStack
+
+import concourse.mybir as mybir
+from concourse.masks import make_identity
+
+K, T, J, R, L, N = 1024, 1024, 256, 512, 512, 256
+FLOPS = 2 * (K * R * J + L * R * J + R * J * N)
+
+F32 = mybir.dt.float32
+BF16 = mybir.dt.bfloat16
+I32 = mybir.dt.int32
+U16 = mybir.dt.uint16
+U8 = mybir.dt.uint8
+E4M3 = mybir.dt.float8_e4m3fn_x4
+E5M2 = mybir.dt.float8_e5m2_x4
+E2M1 = mybir.dt.float4_e2m1fn_x4
+ALU = mybir.AluOpType
+ACT = mybir.ActivationFunctionType
+
+P = 128
+PACK = 4
+PASSES = K // (P * PACK)
+HALVES = J // P
+W_CHUNKS = 2
+W_COLS = R // W_CHUNKS
+W_M = W_COLS // PACK
+VECTOR_GATHERS = {(0, 0), (0, 3), (1, 3)}
+
+
+def tile_list_largerpicks_rival_rowshares_kernel(
+    tc, xf, fk, w, sx_words, sx_scales, ws_words, ws_scales, wb_words, wb_scales, bi, offs, offs2, out
+):
+    nc = tc.nc
+    with ExitStack() as ctx:
+        sb = ctx.enter_context(tc.tile_pool(name="sb", bufs=1))
+        ps = ctx.enter_context(tc.psum_pool(name="ps", bufs=1))
+
+        def tile(shape, dtype, name):
+            return sb.tile(shape, dtype, name=name, align_bytes=64)
+
+        list_a = tile([P, J // 16], U16, "list_a")
+        list_b = tile([P, J // 16], U16, "list_b")
+
+        planes = tile([P, R + J + N], U8, "planes")
+        nc.vector.memset(planes[:].bitcast(I32), 0)
+        ident = tile([P, P], F32, "ident")
+        make_identity(nc, ident[:])
+        ws_cols, sx_cols, wb_cols = slice(0, R), slice(R, R + J), slice(R + J, R + J + N)
+
+        x_rows = xf.rearrange("(g p i) t -> g i p t", g=PASSES, i=PACK)
+        x = {(g, i): tile([P, T], F32, f"x{g}{i}") for g in range(PASSES) for i in range(PACK)}
+        picked_a = [tile([P, PACK, J], F32, f"picked_a{g}") for g in range(PASSES)]
+        picked_b = [tile([P, PACK, J], F32, f"picked_b{g}") for g in range(PASSES)]
+        larger = [tile([P, PACK, J], F32, f"larger{g}") for g in range(PASSES)]
+        u_rows = [tile([P, PACK, J], BF16, f"u_rows{g}") for g in range(PASSES)]
+        u_woven = [tile([P, J, PACK], BF16, f"u_woven{g}") for g in range(PASSES)]
+        u_codes = [tile([P, J], I32, f"u_codes{g}") for g in range(PASSES)]
+        u_scale = [tile([P, J], U8, f"u_scale{g}") for g in range(PASSES)]
+        fk_sb = tile([P, PASSES, PACK], F32, "fk_sb")
+        bi_col = tile([P, 2], F32, "bi_col")
+        bi_all = tile([P, N], F32, "bi_all")
+        ws_raw = tile([P, R], I32, "ws_raw")
+        ws_codes = tile([P, R], I32, "ws_codes")
+        ws_scale = tile([P, R], U8, "ws_scale")
+        sx_codes = tile([P, J], I32, "sx_codes")
+        wb_codes = tile([P, 2 * N], U8, "wb_codes")
+        w_rows = w.rearrange("(g p i) r -> g p i r", g=PASSES, i=PACK)
+        w_raw = {(g, c): tile([P, PACK, W_COLS], F32, f"w_raw{g}{c}") for g in range(PASSES) for c in range(W_CHUNKS)}
+        w_woven = [tile([P, PACK, P, PACK], BF16, f"w_woven{g}") for g in range(PASSES)]
+        w_codes = [tile([P, R], I32, f"w_codes{g}") for g in range(PASSES)]
+        w_scale = [tile([P, R], U8, f"w_scale{g}") for g in range(PASSES)]
+        b2_sb = [tile([P, P, PACK], F32, f"b2_sb{h}") for h in range(HALVES)]
+        a_ps = [ps.tile([P, PACK, P], F32, name=f"a_ps{h}") for h in range(HALVES)]
+        b2_ps = [ps.tile([P, PACK, P], F32, name=f"b2_ps{h}") for h in range(HALVES)]
+        p_ps = [ps.tile([P, N], F32, name=f"p_ps{h}") for h in range(HALVES)]
+        bi_ps = ps.tile([P, 2, P], F32, name="bi_ps")
+
+        def load_x(g, i):
+            nc.sync.dma_start(x[g, i][:], x_rows[g, i])
+
+        def pick(g, i):
+            window = x[g, i][:]
+            nc.scalar.activation(picked_a[g][:, i, :], window.indirect(list_a[:]), ACT.Copy)
+            if (g, i) in VECTOR_GATHERS:
+                nc.vector.tensor_copy(picked_b[g][:, i, :], window.indirect(list_b[:]))
+            else:
+                nc.scalar.activation(picked_b[g][:, i, :], window.indirect(list_b[:]), ACT.Copy)
+
+        def keep_larger(g, i):
+            nc.vector.tensor_tensor(larger[g][:, i, :], picked_a[g][:, i, :], picked_b[g][:, i, :], ALU.max)
+
+        def scale_row(g, i):
+            nc.vector.tensor_scalar(u_rows[g][:, i, :], larger[g][:, i, :], fk_sb[:, g, i : i + 1], None, ALU.mult)
+
+        def quantize_u(g):
+            nc.vector.tensor_copy(
+                u_woven[g][:].rearrange("p (c e) i -> p c i e", e=4),
+                u_rows[g][:].rearrange("p i (c e) -> p c i e", e=4),
+            )
+            nc.vector.quantize_mx(
+                u_codes[g][:].bitcast(E4M3), u_scale[g][:], u_woven[g][:].rearrange("p j i -> p (j i)")
+            )
+
+        def load_w(g, c):
+            nc.sync.dma_start(w_raw[g, c][:], w_rows[g][:, :, c * W_COLS : (c + 1) * W_COLS])
+
+        def weave_w(g, c, copy):
+            copy(
+                w_woven[g][:, :, c * W_M : (c + 1) * W_M, :].rearrange("p t m i -> p m i t"),
+                w_raw[g, c][:].rearrange("p i (m t) -> p m i t", t=PACK),
+            )
+
+        def quantize_w(g, first, count):
+            nc.vector.quantize_mx(
+                w_codes[g][:, first : first + count].bitcast(E5M2),
+                w_scale[g][:, first : first + count],
+                w_woven[g][:].rearrange("p t m i -> p (t m i)")[:, PACK * first : PACK * (first + count)],
+            )
+
+        def first_product(g):
+            for t in range(PACK):
+                cols = slice(t * P, (t + 1) * P)
+                for h in range(HALVES):
+                    slots = slice(h * P, (h + 1) * P)
+                    nc.tensor.matmul_mx(
+                        a_ps[h][:, t, :],
+                        lhsT=w_codes[g][:, cols].bitcast(E5M2),
+                        lhsT_scale=w_scale[g][:, cols],
+                        rhs=u_codes[g][:, slots].bitcast(E4M3),
+                        rhs_scale=u_scale[g][:, slots],
+                        start=(g == 0 and t == 0),
+                        stop=(g == PASSES - 1 and t == PACK - 1),
+                    )
+
+        load_x(0, 0)
+        nc.sync.dma_start(list_a[:], offs)
+        nc.sync.dma_start(list_b[:], offs2)
+        load_x(0, 1)
+        nc.sync.dma_start(fk_sb[:], fk.rearrange("(g p i) o -> p g (i o)", g=PASSES, i=PACK))
+        load_x(0, 2)
+        load_x(0, 3)
+        for cols, scales in ((ws_cols, ws_scales), (sx_cols, sx_scales), (wb_cols, wb_scales)):
+            nc.sync.dma_start(planes[0:16, cols].bitcast(I32), scales[0].bitcast(I32))
+        load_x(1, 0)
+        load_x(1, 1)
+        nc.sync.dma_start(bi_col[:], bi[0].rearrange("(p c) -> p c", c=2))
+        load_x(1, 2)
+        load_x(1, 3)
+        load_w(0, 0)
+        load_w(0, 1)
+        for q in range(1, 4):
+            nc.sync.dma_start(planes[32 * q : 32 * q + 4, :].bitcast(I32), planes[4 * q : 4 * q + 4, :].bitcast(I32))
+        nc.sync.dma_start(ws_raw[:], ws_words[0].rearrange("p n t -> p (n t)").bitcast(I32))
+        nc.sync.dma_start(sx_codes[:], sx_words[0].rearrange("p n t -> p (n t)").bitcast(I32))
+        load_w(1, 0)
+        load_w(1, 1)
+        nc.sync.dma_start(wb_codes[:].bitcast(I32), wb_words[0].bitcast(I32))
+
+        for i in range(PACK):
+            pick(0, i)
+            keep_larger(0, i)
+            scale_row(0, i)
+        quantize_u(0)
+
+        for c in range(2):
+            nc.tensor.transpose(bi_ps[:, c, :], bi_col[:, c : c + 1].to_broadcast([P, P]), ident[:])
+
+        for i in range(PACK):
+            pick(1, i)
+            keep_larger(1, i)
+            scale_row(1, i)
+        quantize_u(1)
+
+        nc.vector.tensor_copy(
+            ws_scale[:].rearrange("p (t m) -> p t m", t=PACK),
+            planes[:, ws_cols].rearrange("p (m t) -> p t m", t=PACK),
+        )
+        nc.scalar.copy(bi_all[:].rearrange("q (p c) -> q p c", c=2), bi_ps[:].rearrange("q c p -> q p c"))
+
+        for c in range(W_CHUNKS):
+            weave_w(0, c, nc.scalar.copy)
+        quantize_w(0, 0, R)
+        first_product(0)
+        nc.vector.tensor_copy(
+            ws_codes[:].rearrange("p (t c e) -> p c t e", t=PACK, e=4),
+            ws_raw[:].rearrange("p (c e t) -> p c t e", t=PACK, e=4),
+        )
+        for c in range(W_CHUNKS):
+            weave_w(1, c, nc.vector.tensor_copy if c == W_CHUNKS - 1 else nc.scalar.copy)
+            for t in range(PACK):
+                quantize_w(1, t * P + c * W_M, W_M)
+
+        for h in range(HALVES):
+            slots = slice(h * P, (h + 1) * P)
+            for t in range(PACK):
+                cols = slice(t * P, (t + 1) * P)
+                nc.tensor.matmul_mx(
+                    b2_ps[h][:, t, :],
+                    lhsT=ws_codes[:, cols].bitcast(E5M2),
+                    lhsT_scale=ws_scale[:, cols],
+                    rhs=sx_codes[:, slots].bitcast(E5M2),
+                    rhs_scale=planes[:, R + h * P : R + (h + 1) * P],
+                    start=True,
+                    stop=True,
+                )
+            nc.scalar.copy(b2_sb[h][:], b2_ps[h][:].rearrange("p t j -> p j t"))
+        first_product(1)
+
+        hid = [tile([P, P, PACK], BF16, f"hid{h}") for h in range(HALVES)]
+        hid_codes = [tile([P, P], I32, f"hid_codes{h}") for h in range(HALVES)]
+        hid_scale = [tile([P, P], U8, f"hid_scale{h}") for h in range(HALVES)]
+        neg_z = [tile([P, N], F32, f"neg_z{h}") for h in range(HALVES)]
+        ea = [tile([P, N], F32, f"ea{h}") for h in range(HALVES)]
+        y = [tile([P, N], F32, f"y{h}") for h in range(HALVES)]
+        neg_top = [tile([P, 1], F32, f"neg_top{h}") for h in range(HALVES)]
+        total = [tile([P, 1], F32, f"total{h}") for h in range(HALVES)]
+        inverse = [tile([P, 1], F32, f"inverse{h}") for h in range(HALVES)]
+
+        for h in range(HALVES):
+            nc.vector.tensor_tensor(hid[h][:], a_ps[h][:].rearrange("p t j -> p j t"), b2_sb[h][:], ALU.max)
+            nc.vector.quantize_mx(
+                hid_codes[h][:].bitcast(E5M2), hid_scale[h][:], hid[h][:].rearrange("p j t -> p (j t)")
+            )
+            nc.tensor.matmul_mx(
+                p_ps[h][:],
+                lhsT=hid_codes[h][:].bitcast(E5M2),
+                lhsT_scale=hid_scale[h][:],
+                rhs=wb_codes[:].bitcast(E2M1),
+                rhs_scale=planes[:, wb_cols],
+                start=True,
+                stop=True,
+            )
+        for h in range(HALVES):
+            nc.vector.scalar_tensor_tensor(neg_z[h][:], p_ps[h][:], -0.7, bi_all[:], ALU.mult, ALU.subtract)
+            nc.vector.tensor_reduce(neg_top[h][:], neg_z[h][:], mybir.AxisListType.X, ALU.min)
+            nc.scalar.activation(
+                ea[h][:], neg_z[h][:], ACT.Exp, bias=neg_top[h][:], scale=-1.0, accum_out=total[h][:]
+            )
+        for h in range(HALVES):
+            nc.vector.reciprocal(inverse[h][:], total[h][:])
+            nc.vector.tensor_scalar(y[h][:], ea[h][:], inverse[h][:], 256.0, ALU.mult, ALU.mult)
+            nc.sync.dma_start(out[h * P : (h + 1) * P, :], y[h][:])

@@ -43,6 +43,9 @@ def tile_list_largerpicks_rival_rowshares_kernel(
 
         planes = tile([P, R + J + N], U8, "planes")
         nc.vector.memset(planes[:].bitcast(I32), 0)
+        warm = tile([P, 2], F32, "warm")
+        nc.vector.memset(warm[:, 0:1], 0.0)
+        nc.scalar.activation(warm[:, 1:2], warm[:, 0:1], ACT.Exp)
         ident = tile([P, P], F32, "ident")
         make_identity(nc, ident[:])
         ws_cols, sx_cols, wb_cols = slice(0, R), slice(R, R + J), slice(R + J, R + J + N)
@@ -118,10 +121,10 @@ def tile_list_largerpicks_rival_rowshares_kernel(
             )
 
         def first_product(g):
-            for t in range(PACK):
-                cols = slice(t * P, (t + 1) * P)
-                for h in range(HALVES):
-                    slots = slice(h * P, (h + 1) * P)
+            for h in range(HALVES):
+                slots = slice(h * P, (h + 1) * P)
+                for t in range(PACK):
+                    cols = slice(t * P, (t + 1) * P)
                     nc.tensor.matmul_mx(
                         a_ps[h][:, t, :],
                         lhsT=w_codes[g][:, cols].bitcast(E5M2),
@@ -151,9 +154,9 @@ def tile_list_largerpicks_rival_rowshares_kernel(
         for q in range(1, 4):
             nc.sync.dma_start(planes[32 * q : 32 * q + 4, :].bitcast(I32), planes[4 * q : 4 * q + 4, :].bitcast(I32))
         nc.sync.dma_start(ws_raw[:], ws_words[0].rearrange("p n t -> p (n t)").bitcast(I32))
-        nc.sync.dma_start(sx_codes[:], sx_words[0].rearrange("p n t -> p (n t)").bitcast(I32))
         load_w(1, 0)
         load_w(1, 1)
+        nc.sync.dma_start(sx_codes[:], sx_words[0].rearrange("p n t -> p (n t)").bitcast(I32))
         nc.sync.dma_start(wb_codes[:].bitcast(I32), wb_words[0].bitcast(I32))
 
         for i in range(PACK):

@@ -24,6 +24,7 @@ HALVES = J // P
 W_CHUNKS = 2
 W_COLS = R // W_CHUNKS
 W_M = W_COLS // PACK
+SCALAR_M = 96
 VECTOR_GATHERS = {(0, 0), (0, 3), (1, 3)}
 
 
@@ -42,7 +43,9 @@ def tile_list_largerpicks_rival_rowshares_kernel(
         list_b = tile([P, J // 16], U16, "list_b")
 
         planes = tile([P, R + J + N], U8, "planes")
-        nc.vector.memset(planes[:].bitcast(I32), 0)
+        ws_rows = tile([P, R], U8, "ws_rows")
+        nc.vector.memset(ws_rows[:].bitcast(I32), 0)
+        nc.vector.memset(planes[:, R:].bitcast(I32), 0)
         warm = tile([P, 2], F32, "warm")
         nc.vector.memset(warm[:, 0:1], 0.0)
         nc.scalar.activation(warm[:, 1:2], warm[:, 0:1], ACT.Exp)
@@ -55,7 +58,6 @@ def tile_list_largerpicks_rival_rowshares_kernel(
         picked_a = [tile([P, PACK, J], F32, f"picked_a{g}") for g in range(PASSES)]
         picked_b = [tile([P, PACK, J], F32, f"picked_b{g}") for g in range(PASSES)]
         larger = [tile([P, PACK, J], F32, f"larger{g}") for g in range(PASSES)]
-        u_rows = [tile([P, PACK, J], BF16, f"u_rows{g}") for g in range(PASSES)]
         u_woven = [tile([P, J, PACK], BF16, f"u_woven{g}") for g in range(PASSES)]
         u_codes = [tile([P, J], I32, f"u_codes{g}") for g in range(PASSES)]
         u_scale = [tile([P, J], U8, f"u_scale{g}") for g in range(PASSES)]
@@ -64,15 +66,14 @@ def tile_list_largerpicks_rival_rowshares_kernel(
         bi_all = tile([P, N], F32, "bi_all")
         ws_raw = tile([P, R], I32, "ws_raw")
         ws_codes = tile([P, R], I32, "ws_codes")
-        ws_scale = tile([P, R], U8, "ws_scale")
         sx_codes = tile([P, J], I32, "sx_codes")
         wb_codes = tile([P, 2 * N], U8, "wb_codes")
         w_rows = w.rearrange("(g p i) r -> g p i r", g=PASSES, i=PACK)
-        w_raw = {(g, c): tile([P, PACK, W_COLS], F32, f"w_raw{g}{c}") for g in range(PASSES) for c in range(W_CHUNKS)}
+        w_first = tile([P, PACK, R], F32, "w_first")
+        w_last = [tile([P, PACK, W_COLS], F32, f"w_last{c}") for c in range(W_CHUNKS)]
         w_woven = [tile([P, PACK, P, PACK], BF16, f"w_woven{g}") for g in range(PASSES)]
         w_codes = [tile([P, R], I32, f"w_codes{g}") for g in range(PASSES)]
         w_scale = [tile([P, R], U8, f"w_scale{g}") for g in range(PASSES)]
-        b2_sb = [tile([P, P, PACK], F32, f"b2_sb{h}") for h in range(HALVES)]
         a_ps = [ps.tile([P, PACK, P], F32, name=f"a_ps{h}") for h in range(HALVES)]
         b2_ps = [ps.tile([P, PACK, P], F32, name=f"b2_ps{h}") for h in range(HALVES)]
         p_ps = [ps.tile([P, N], F32, name=f"p_ps{h}") for h in range(HALVES)]
@@ -92,25 +93,25 @@ def tile_list_largerpicks_rival_rowshares_kernel(
         def keep_larger(g, i):
             nc.vector.tensor_tensor(larger[g][:, i, :], picked_a[g][:, i, :], picked_b[g][:, i, :], ALU.max)
 
-        def scale_row(g, i):
-            nc.vector.tensor_scalar(u_rows[g][:, i, :], larger[g][:, i, :], fk_sb[:, g, i : i + 1], None, ALU.mult)
-
         def quantize_u(g):
-            nc.vector.tensor_copy(
+            nc.vector.tensor_tensor(
                 u_woven[g][:].rearrange("p (c e) i -> p c i e", e=4),
-                u_rows[g][:].rearrange("p i (c e) -> p c i e", e=4),
+                larger[g][:].rearrange("p i (c e) -> p c i e", e=4),
+                fk_sb[:, g, :].unsqueeze(1).unsqueeze(3).to_broadcast([P, J // 4, PACK, 4]),
+                ALU.mult,
             )
             nc.vector.quantize_mx(
                 u_codes[g][:].bitcast(E4M3), u_scale[g][:], u_woven[g][:].rearrange("p j i -> p (j i)")
             )
 
-        def load_w(g, c):
-            nc.sync.dma_start(w_raw[g, c][:], w_rows[g][:, :, c * W_COLS : (c + 1) * W_COLS])
+        def load_w_last(c):
+            nc.sync.dma_start(w_last[c][:], w_rows[1][:, :, c * W_COLS : (c + 1) * W_COLS])
 
-        def weave_w(g, c, copy):
+        def weave_w(g, first, raw, copy):
+            count = raw.shape[2] // PACK
             copy(
-                w_woven[g][:, :, c * W_M : (c + 1) * W_M, :].rearrange("p t m i -> p m i t"),
-                w_raw[g, c][:].rearrange("p i (m t) -> p m i t", t=PACK),
+                w_woven[g][:, :, first : first + count, :].rearrange("p t m i -> p m i t"),
+                raw.rearrange("p i (m t) -> p m i t", t=PACK),
             )
 
         def quantize_w(g, first, count):
@@ -142,27 +143,30 @@ def tile_list_largerpicks_rival_rowshares_kernel(
         nc.sync.dma_start(fk_sb[:], fk.rearrange("(g p i) o -> p g (i o)", g=PASSES, i=PACK))
         load_x(0, 2)
         load_x(0, 3)
-        for cols, scales in ((ws_cols, ws_scales), (sx_cols, sx_scales), (wb_cols, wb_scales)):
+        nc.sync.dma_start(ws_rows[0:16, :].bitcast(I32), ws_scales[0].bitcast(I32))
+        for cols, scales in ((sx_cols, sx_scales), (wb_cols, wb_scales)):
             nc.sync.dma_start(planes[0:16, cols].bitcast(I32), scales[0].bitcast(I32))
+        nc.vector.tensor_copy(
+            planes[:, ws_cols].rearrange("p (t m) -> p t m", t=PACK),
+            ws_rows[:].rearrange("p (m t) -> p t m", t=PACK),
+        )
         load_x(1, 0)
         load_x(1, 1)
         nc.sync.dma_start(bi_col[:], bi[0].rearrange("(p c) -> p c", c=2))
         load_x(1, 2)
         load_x(1, 3)
-        load_w(0, 0)
-        load_w(0, 1)
         for q in range(1, 4):
             nc.sync.dma_start(planes[32 * q : 32 * q + 4, :].bitcast(I32), planes[4 * q : 4 * q + 4, :].bitcast(I32))
         nc.sync.dma_start(ws_raw[:], ws_words[0].rearrange("p n t -> p (n t)").bitcast(I32))
-        load_w(1, 0)
-        load_w(1, 1)
         nc.sync.dma_start(sx_codes[:], sx_words[0].rearrange("p n t -> p (n t)").bitcast(I32))
+        nc.sync.dma_start(w_first[:], w_rows[0])
+        load_w_last(0)
+        load_w_last(1)
         nc.sync.dma_start(wb_codes[:].bitcast(I32), wb_words[0].bitcast(I32))
 
         for i in range(PACK):
             pick(0, i)
             keep_larger(0, i)
-            scale_row(0, i)
         quantize_u(0)
 
         for c in range(2):
@@ -171,28 +175,14 @@ def tile_list_largerpicks_rival_rowshares_kernel(
         for i in range(PACK):
             pick(1, i)
             keep_larger(1, i)
-            scale_row(1, i)
         quantize_u(1)
 
-        nc.vector.tensor_copy(
-            ws_scale[:].rearrange("p (t m) -> p t m", t=PACK),
-            planes[:, ws_cols].rearrange("p (m t) -> p t m", t=PACK),
-        )
         nc.scalar.copy(bi_all[:].rearrange("q (p c) -> q p c", c=2), bi_ps[:].rearrange("q c p -> q p c"))
 
-        for c in range(W_CHUNKS):
-            weave_w(0, c, nc.scalar.copy)
-        quantize_w(0, 0, R)
-        first_product(0)
         nc.vector.tensor_copy(
             ws_codes[:].rearrange("p (t c e) -> p c t e", t=PACK, e=4),
             ws_raw[:].rearrange("p (c e t) -> p c t e", t=PACK, e=4),
         )
-        for c in range(W_CHUNKS):
-            weave_w(1, c, nc.vector.tensor_copy if c == W_CHUNKS - 1 else nc.scalar.copy)
-            for t in range(PACK):
-                quantize_w(1, t * P + c * W_M, W_M)
-
         for h in range(HALVES):
             slots = slice(h * P, (h + 1) * P)
             for t in range(PACK):
@@ -200,13 +190,24 @@ def tile_list_largerpicks_rival_rowshares_kernel(
                 nc.tensor.matmul_mx(
                     b2_ps[h][:, t, :],
                     lhsT=ws_codes[:, cols].bitcast(E5M2),
-                    lhsT_scale=ws_scale[:, cols],
+                    lhsT_scale=planes[:, cols],
                     rhs=sx_codes[:, slots].bitcast(E5M2),
                     rhs_scale=planes[:, R + h * P : R + (h + 1) * P],
                     start=True,
                     stop=True,
                 )
-            nc.scalar.copy(b2_sb[h][:], b2_ps[h][:].rearrange("p t j -> p j t"))
+        weave_w(0, 0, w_first[:, :, : PACK * SCALAR_M], nc.scalar.copy)
+        weave_w(0, SCALAR_M, w_first[:, :, PACK * SCALAR_M :], nc.vector.tensor_copy)
+        quantize_w(0, 0, R)
+        first_product(0)
+        for c in range(W_CHUNKS):
+            weave_w(1, c * W_M, w_last[c][:], nc.vector.tensor_copy if c == W_CHUNKS - 1 else nc.scalar.copy)
+            for t in range(PACK):
+                quantize_w(1, t * P + c * W_M, W_M)
+
+        b2_sb = sb.tile([P, HALVES, P, PACK], F32, name="b2_sb", tag="w_last0", align_bytes=64)
+        for h in range(HALVES):
+            nc.scalar.copy(b2_sb[:, h], b2_ps[h][:].rearrange("p t j -> p j t"))
         first_product(1)
 
         hid = [tile([P, P, PACK], BF16, f"hid{h}") for h in range(HALVES)]
@@ -220,7 +221,7 @@ def tile_list_largerpicks_rival_rowshares_kernel(
         inverse = [tile([P, 1], F32, f"inverse{h}") for h in range(HALVES)]
 
         for h in range(HALVES):
-            nc.vector.tensor_tensor(hid[h][:], a_ps[h][:].rearrange("p t j -> p j t"), b2_sb[h][:], ALU.max)
+            nc.vector.tensor_tensor(hid[h][:], a_ps[h][:].rearrange("p t j -> p j t"), b2_sb[:, h], ALU.max)
             nc.vector.quantize_mx(
                 hid_codes[h][:].bitcast(E5M2), hid_scale[h][:], hid[h][:].rearrange("p j t -> p (j t)")
             )

from contextlib import ExitStack

import concourse.mybir as mybir
from concourse.masks import make_identity

K, T, J, R, L, N = 1024, 1024, 256, 512, 512, 256
FLOPS = 2 * (K * R * J + L * R * J + R * J * N)

F32 = mybir.dt.float32
BF16 = mybir.dt.bfloat16
I32 = mybir.dt.int32
U16 = mybir.dt.uint16
U8 = mybir.dt.uint8
E4M3 = mybir.dt.float8_e4m3fn_x4
E5M2 = mybir.dt.float8_e5m2_x4
E2M1 = mybir.dt.float4_e2m1fn_x4
ALU = mybir.AluOpType
ACT = mybir.ActivationFunctionType

P = 128
PACK = 4
PASSES = K // (P * PACK)
HALVES = J // P
W_CHUNKS = 2
W_COLS = R // W_CHUNKS
W_M = W_COLS // PACK
SCALAR_M = 96
VECTOR_GATHERS = {(0, 0), (0, 3), (1, 3)}


def tile_list_largerpicks_rival_rowshares_kernel(
    tc, xf, fk, w, sx_words, sx_scales, ws_words, ws_scales, wb_words, wb_scales, bi, offs, offs2, out
):
    nc = tc.nc
    with ExitStack() as ctx:
        sb = ctx.enter_context(tc.tile_pool(name="sb", bufs=1))
        ps = ctx.enter_context(tc.psum_pool(name="ps", bufs=1))

        def tile(shape, dtype, name):
            return sb.tile(shape, dtype, name=name, align_bytes=64)

        list_a = tile([P, J // 16], U16, "list_a")
        list_b = tile([P, J // 16], U16, "list_b")

        planes = tile([P, R + J + N], U8, "planes")
        ws_rows = tile([P, R], U8, "ws_rows")
        nc.vector.memset(ws_rows[:].bitcast(I32), 0)
        nc.vector.memset(planes[:, R:].bitcast(I32), 0)
        warm = tile([P, 2], F32, "warm")
        nc.vector.memset(warm[:, 0:1], 0.0)
        nc.scalar.activation(warm[:, 1:2], warm[:, 0:1], ACT.Exp)
        ident = tile([P, P], F32, "ident")
        make_identity(nc, ident[:])
        ws_cols, sx_cols, wb_cols = slice(0, R), slice(R, R + J), slice(R + J, R + J + N)

        x_rows = xf.rearrange("(g p i) t -> g i p t", g=PASSES, i=PACK)
        x = {(g, i): tile([P, T], F32, f"x{g}{i}") for g in range(PASSES) for i in range(PACK)}
        picked_a = [tile([P, PACK, J], F32, f"picked_a{g}") for g in range(PASSES)]
        picked_b = [tile([P, PACK, J], F32, f"picked_b{g}") for g in range(PASSES)]
        larger = [tile([P, PACK, J], F32, f"larger{g}") for g in range(PASSES)]
        u_woven = [tile([P, J, PACK], BF16, f"u_woven{g}") for g in range(PASSES)]
        u_codes = [tile([P, J], I32, f"u_codes{g}") for g in range(PASSES)]
        u_scale = [tile([P, J], U8, f"u_scale{g}") for g in range(PASSES)]
        fk_sb = tile([P, PASSES, PACK], F32, "fk_sb")
        bi_col = tile([P, 2], F32, "bi_col")
        bi_all = tile([P, N], F32, "bi_all")
        ws_raw = tile([P, R], I32, "ws_raw")
        ws_codes = tile([P, R], I32, "ws_codes")
        sx_codes = tile([P, J], I32, "sx_codes")
        wb_codes = tile([P, 2 * N], U8, "wb_codes")
        w_rows = w.rearrange("(g p i) r -> g p i r", g=PASSES, i=PACK)
        w_first = tile([P, PACK, R], F32, "w_first")
        w_last = [tile([P, PACK, W_COLS], F32, f"w_last{c}") for c in range(W_CHUNKS)]
        w_woven = [tile([P, PACK, P, PACK], BF16, f"w_woven{g}") for g in range(PASSES)]
        w_codes = [tile([P, R], I32, f"w_codes{g}") for g in range(PASSES)]
        w_scale = [tile([P, R], U8, f"w_scale{g}") for g in range(PASSES)]
        a_ps = [ps.tile([P, PACK, P], F32, name=f"a_ps{h}") for h in range(HALVES)]
        b2_ps = [ps.tile([P, PACK, P], F32, name=f"b2_ps{h}") for h in range(HALVES)]
        p_ps = [ps.tile([P, N], F32, name=f"p_ps{h}") for h in range(HALVES)]
        bi_ps = ps.tile([P, 2, P], F32, name="bi_ps")

        def load_x(g, i):
            nc.sync.dma_start(x[g, i][:], x_rows[g, i])

        def pick(g, i):
            window = x[g, i][:]
            nc.scalar.activation(picked_a[g][:, i, :], window.indirect(list_a[:]), ACT.Copy)
            if (g, i) in VECTOR_GATHERS:
                nc.vector.tensor_copy(picked_b[g][:, i, :], window.indirect(list_b[:]))
            else:
                nc.scalar.activation(picked_b[g][:, i, :], window.indirect(list_b[:]), ACT.Copy)

        def keep_larger(g, i):
            nc.vector.tensor_tensor(larger[g][:, i, :], picked_a[g][:, i, :], picked_b[g][:, i, :], ALU.max)

        def quantize_u(g):
            nc.vector.tensor_tensor(
                u_woven[g][:].rearrange("p (c e) i -> p c i e", e=4),
                larger[g][:].rearrange("p i (c e) -> p c i e", e=4),
                fk_sb[:, g, :].unsqueeze(1).unsqueeze(3).to_broadcast([P, J // 4, PACK, 4]),
                ALU.mult,
            )
            nc.vector.quantize_mx(
                u_codes[g][:].bitcast(E4M3), u_scale[g][:], u_woven[g][:].rearrange("p j i -> p (j i)")
            )

        def load_w_last(c):
            nc.sync.dma_start(w_last[c][:], w_rows[1][:, :, c * W_COLS : (c + 1) * W_COLS])

        def weave_w(g, first, raw, copy):
            count = raw.shape[2] // PACK
            copy(
                w_woven[g][:, :, first : first + count, :].rearrange("p t m i -> p m i t"),
                raw.rearrange("p i (m t) -> p m i t", t=PACK),
            )

        def quantize_w(g, first, count):
            nc.vector.quantize_mx(
                w_codes[g][:, first : first + count].bitcast(E5M2),
                w_scale[g][:, first : first + count],
                w_woven[g][:].rearrange("p t m i -> p (t m i)")[:, PACK * first : PACK * (first + count)],
            )

        def first_product(g):
            for h in range(HALVES):
                slots = slice(h * P, (h + 1) * P)
                for t in range(PACK):
                    cols = slice(t * P, (t + 1) * P)
                    nc.tensor.matmul_mx(
                        a_ps[h][:, t, :],
                        lhsT=w_codes[g][:, cols].bitcast(E5M2),
                        lhsT_scale=w_scale[g][:, cols],
                        rhs=u_codes[g][:, slots].bitcast(E4M3),
                        rhs_scale=u_scale[g][:, slots],
                        start=(g == 0 and t == 0),
                        stop=(g == PASSES - 1 and t == PACK - 1),
                    )

        load_x(0, 0)
        nc.sync.dma_start(list_a[:], offs)
        nc.sync.dma_start(list_b[:], offs2)
        load_x(0, 1)
        nc.sync.dma_start(fk_sb[:], fk.rearrange("(g p i) o -> p g (i o)", g=PASSES, i=PACK))
        load_x(0, 2)
        load_x(0, 3)
        nc.sync.dma_start(ws_rows[0:16, :].bitcast(I32), ws_scales[0].bitcast(I32))
        for cols, scales in ((sx_cols, sx_scales), (wb_cols, wb_scales)):
            nc.sync.dma_start(planes[0:16, cols].bitcast(I32), scales[0].bitcast(I32))
        nc.vector.tensor_copy(
            planes[:, ws_cols].rearrange("p (t m) -> p t m", t=PACK),
            ws_rows[:].rearrange("p (m t) -> p t m", t=PACK),
        )
        load_x(1, 0)
        load_x(1, 1)
        nc.sync.dma_start(bi_col[:], bi[0].rearrange("(p c) -> p c", c=2))
        load_x(1, 2)
        load_x(1, 3)
        for q in range(1, 4):
            nc.sync.dma_start(planes[32 * q : 32 * q + 4, :].bitcast(I32), planes[4 * q : 4 * q + 4, :].bitcast(I32))
        nc.sync.dma_start(ws_raw[:], ws_words[0].rearrange("p n t -> p (n t)").bitcast(I32))
        nc.sync.dma_start(sx_codes[:], sx_words[0].rearrange("p n t -> p (n t)").bitcast(I32))
        nc.sync.dma_start(w_first[:], w_rows[0])
        load_w_last(0)
        load_w_last(1)
        nc.sync.dma_start(wb_codes[:].bitcast(I32), wb_words[0].bitcast(I32))

        for i in range(PACK):
            pick(0, i)
            keep_larger(0, i)
        quantize_u(0)

        for c in range(2):
            nc.tensor.transpose(bi_ps[:, c, :], bi_col[:, c : c + 1].to_broadcast([P, P]), ident[:])

        for i in range(PACK):
            pick(1, i)
            keep_larger(1, i)
        quantize_u(1)

        nc.scalar.copy(bi_all[:].rearrange("q (p c) -> q p c", c=2), bi_ps[:].rearrange("q c p -> q p c"))

        nc.vector.tensor_copy(
            ws_codes[:].rearrange("p (t c e) -> p c t e", t=PACK, e=4),
            ws_raw[:].rearrange("p (c e t) -> p c t e", t=PACK, e=4),
        )
        for h in range(HALVES):
            slots = slice(h * P, (h + 1) * P)
            for t in range(PACK):
                cols = slice(t * P, (t + 1) * P)
                nc.tensor.matmul_mx(
                    b2_ps[h][:, t, :],
                    lhsT=ws_codes[:, cols].bitcast(E5M2),
                    lhsT_scale=planes[:, cols],
                    rhs=sx_codes[:, slots].bitcast(E5M2),
                    rhs_scale=planes[:, R + h * P : R + (h + 1) * P],
                    start=True,
                    stop=True,
                )
        weave_w(0, 0, w_first[:, :, : PACK * SCALAR_M], nc.scalar.copy)
        weave_w(0, SCALAR_M, w_first[:, :, PACK * SCALAR_M :], nc.vector.tensor_copy)
        quantize_w(0, 0, R)
        first_product(0)
        for c in range(W_CHUNKS):
            weave_w(1, c * W_M, w_last[c][:], nc.vector.tensor_copy if c == W_CHUNKS - 1 else nc.scalar.copy)
            for t in range(PACK):
                quantize_w(1, t * P + c * W_M, W_M)

        b2_sb = sb.tile([P, HALVES, P, PACK], F32, name="b2_sb", tag="w_last0", align_bytes=64)
        for h in range(HALVES):
            nc.scalar.copy(b2_sb[:, h], b2_ps[h][:].rearrange("p t j -> p j t"))
        first_product(1)

        hid = [tile([P, P, PACK], BF16, f"hid{h}") for h in range(HALVES)]
        hid_codes = [tile([P, P], I32, f"hid_codes{h}") for h in range(HALVES)]
        hid_scale = [tile([P, P], U8, f"hid_scale{h}") for h in range(HALVES)]
        neg_z = [tile([P, N], F32, f"neg_z{h}") for h in range(HALVES)]
        ea = [tile([P, N], F32, f"ea{h}") for h in range(HALVES)]
        y = [tile([P, N], F32, f"y{h}") for h in range(HALVES)]
        neg_top = [tile([P, 1], F32, f"neg_top{h}") for h in range(HALVES)]
        total = [tile([P, 1], F32, f"total{h}") for h in range(HALVES)]
        inverse = [tile([P, 1], F32, f"inverse{h}") for h in range(HALVES)]

        for h in range(HALVES):
            nc.vector.tensor_tensor(hid[h][:], a_ps[h][:].rearrange("p t j -> p j t"), b2_sb[:, h], ALU.max)
            nc.vector.quantize_mx(
                hid_codes[h][:].bitcast(E5M2), hid_scale[h][:], hid[h][:].rearrange("p j t -> p (j t)")
            )
            nc.tensor.matmul_mx(
                p_ps[h][:],
                lhsT=hid_codes[h][:].bitcast(E5M2),
                lhsT_scale=hid_scale[h][:],
                rhs=wb_codes[:].bitcast(E2M1),
                rhs_scale=planes[:, wb_cols],
                start=True,
                stop=True,
            )
        for h in range(HALVES):
            nc.vector.scalar_tensor_tensor(neg_z[h][:], p_ps[h][:], -0.7, bi_all[:], ALU.mult, ALU.subtract)
            nc.vector.tensor_reduce(neg_top[h][:], neg_z[h][:], mybir.AxisListType.X, ALU.min)
            nc.scalar.activation(
                ea[h][:], neg_z[h][:], ACT.Exp, bias=neg_top[h][:], scale=-1.0, accum_out=total[h][:]
            )
        for h in range(HALVES):
            nc.vector.reciprocal(inverse[h][:], total[h][:])
            nc.vector.tensor_scalar(y[h][:], ea[h][:], inverse[h][:], 256.0, ALU.mult, ALU.mult)
            nc.sync.dma_start(out[h * P : (h + 1) * P, :], y[h][:])
